import numpy as np
import ml_dtypes


def mxq(x, axis, fmt="e4m3"):
    dtype, down = {"e4m3": (ml_dtypes.float8_e4m3fn, 7), "e5m2": (ml_dtypes.float8_e5m2, 14)}[fmt]
    v = np.moveaxis(np.asarray(x, np.float32).astype(ml_dtypes.bfloat16).astype(np.float64), axis, -1)
    blocks = v.reshape(v.shape[:-1] + (-1, 32))
    amax = np.abs(blocks).max(-1, keepdims=True)
    byte = np.maximum(np.where(amax > 0, np.frexp(amax)[1] - 1 + 127, 0) - down, 1)
    scale = np.exp2(byte - 127.0)
    codes = (blocks / scale).astype(np.float32).astype(dtype).astype(np.float64)
    return np.moveaxis((codes * scale).reshape(v.shape), -1, axis)


WIDE = False


def mx_kscale(k):
    if not WIDE:
        return np.ones(k)
    levels = np.array([10, -10, 5, -5, 0])
    if k % 512:
        return np.exp2(np.random.permutation(np.resize(levels, k // 32))).repeat(32)
    a = np.empty((k // 512, 16))
    for p in range(k // 512):
        a[p, :8] = np.random.permutation(np.resize(levels, 8))
        for g in range(8):
            far = levels[np.abs(levels - a[p, g]) >= 10]
            a[p, g + 8] = far[np.random.randint(len(far))]
    return np.exp2(a.ravel()).repeat(32)


def f64(x):
    return np.asarray(x).astype(np.float64)


def striped(idx):
    return np.tile(idx.reshape(-1, 16).T, (8, 1)).astype(np.uint16)


def unstriped(offs):
    return offs[:16].T.reshape(-1).astype(np.int64)


def striped8(idx):
    return np.concatenate([x.reshape(-1, 16).T for x in idx]).astype(np.uint16)


def runs(offs, k):
    lists = np.stack([offs[16 * r : 16 * r + 16].T.reshape(-1) for r in range(8)]).astype(np.int64)
    return lists[np.arange(k) % 512 // 64]


def pack_weight(w):
    k, n = w.shape
    w = f64(np.asarray(w, np.float32).astype(ml_dtypes.bfloat16)).reshape(k // 32, 32, n)
    amax = np.abs(w).max(1)
    byte = np.clip(np.where(amax > 0, np.frexp(amax)[1] - 1 + 127 - 7, 1), 1, 254)
    scaled = (w * np.exp2(127.0 - byte)[:, None, :]).reshape(k, n).astype(np.float32)
    words = np.ascontiguousarray(scaled.reshape(k // 512, 128, 4, n).transpose(0, 1, 3, 2)).astype(ml_dtypes.float8_e4m3fn).view(np.uint8)
    return words, np.ascontiguousarray(byte.astype(np.uint8).reshape(k // 512, 16, n))


def unpack_weight(words, scales):
    g, p, n, _ = words.shape
    vals = np.ascontiguousarray(words).view(ml_dtypes.float8_e4m3fn).astype(np.float64) * np.repeat(np.exp2(scales.astype(np.float64) - 127.0), 8, axis=1)[..., None]
    return vals.transpose(0, 1, 3, 2).reshape(g * 512, n)


E2M1 = np.array([0.0, 0.5, 1.0, 1.5, 2.0, 3.0, 4.0, 6.0, -0.0, -0.5, -1.0, -1.5, -2.0, -3.0, -4.0, -6.0])


def pack_fp4(w):
    k, n = w.shape
    w = f64(np.asarray(w, np.float32).astype(ml_dtypes.bfloat16)).reshape(k // 32, 32, n)
    amax = np.abs(w).max(1)
    mant, ex = np.frexp(amax / 6.0)
    byte = np.clip(np.where(amax > 0, np.where(mant > 0.5, ex, ex - 1) + 127, 1), 1, 254)
    scaled = (w * np.exp2(127.0 - byte)[:, None, :]).reshape(k, n).astype(np.float32)
    c = np.ascontiguousarray(scaled.reshape(k // 512, 128, 4, n).transpose(0, 1, 3, 2)).astype(ml_dtypes.float4_e2m1fn).view(np.uint8) & 0xF
    words = (c[..., 0::2] | (c[..., 1::2] << 4)).reshape(k // 512, 128, 2 * n)
    return np.ascontiguousarray(words), np.ascontiguousarray(byte.astype(np.uint8).reshape(k // 512, 16, n))


def unpack_fp4(words, scales):
    g, _, n = scales.shape
    words = np.ascontiguousarray(words).reshape(g, 128, n, 2)
    nib = np.empty((g, 128, n, 4), np.uint8)
    nib[..., 0::2] = words & 0xF
    nib[..., 1::2] = words >> 4
    vals = E2M1[nib] * np.repeat(np.exp2(scales.astype(np.float64) - 127.0), 8, axis=1)[..., None]
    return vals.transpose(0, 1, 3, 2).reshape(g * 512, n)


K, T, S, H, W, G = 512, 1024, 256, 512, 128, 2048


def setup_inputs():
    n = np.random.standard_normal
    s = mx_kscale(K)[:, None]
    packed_xT = pack_weight(n((K, T)) * s)
    packed_w1 = pack_fp4(n((K, H)) / np.sqrt(K) / s)
    packed_dT = pack_weight(n((K, G)) / s)
    perm = np.random.permutation(S)
    return {
        "x_words": packed_xT[0],
        "x_scales": packed_xT[1],
        "w1_words": packed_w1[0],
        "w1_scales": packed_w1[1],
        "gs": (np.random.uniform(0.5, 1.5, (K, 1)) * s).astype(np.float32),
        "d_words": packed_dT[0],
        "d_scales": packed_dT[1],
        "offs": striped(np.random.permutation(T)[:S]),
        "n1": striped(perm[:W]),
        "n2": striped(perm[W:]),
        "k1": striped8(np.random.randint(0, G, (8, H))),
        "k2": striped8(np.random.randint(0, G, (8, H))),
        "two": striped(np.random.permutation(T)[:S]),
        "n3": striped(np.random.permutation(S)),
        "n4": striped(np.random.permutation(S)),
    }


def reference(x_words, x_scales, w1_words, w1_scales, gs, d_words, d_scales, offs, n1, n2, k1, k2, two, n3, n4):
    d_k1 = unpack_weight(d_words, d_scales)[np.arange(K)[:, None], runs(k1, K)]
    xq = unpack_weight(x_words, x_scales)[:, unstriped(offs)]
    y = unpack_fp4(w1_words, w1_scales).T @ xq
    pa = y[:, unstriped(n1)]
    pb = y[:, unstriped(n2)]
    rb = pa - pb
    ra = 0.75 * (pa + pb)
    ds = np.zeros((H, S))
    ds[:, unstriped(n1)] = ra
    dt = ds.copy()
    dt[:, unstriped(n2)] = rb
    z = f64(gs) * dt
    d_k2 = unpack_weight(d_words, d_scales)[np.arange(K)[:, None], runs(k2, K)]
    x_two = unpack_weight(x_words, x_scales)[:, unstriped(two)]
    h = 0.0625 * ((d_k1.T @ mxq(z, 0, "e4m3") + d_k2.T @ x_two))
    st = np.maximum(h, h[:, unstriped(n3)])
    ds2 = np.zeros((H, S))
    ds2[:, unstriped(n4)] = st
    return ds2 - h

@@ -1,0 +1,163 @@
+from contextlib import ExitStack
+
+import concourse.mybir as mybir
+
+K, T, S, H, W, G = 512, 1024, 256, 512, 128, 2048
+P = 128
+PACK = 4
+FLOPS = 3 * 2 * K * H * S
+
+F32 = mybir.dt.float32
+BF16 = mybir.dt.bfloat16
+I32 = mybir.dt.int32
+U32 = mybir.dt.uint32
+U16 = mybir.dt.uint16
+U8 = mybir.dt.uint8
+FP8X4 = mybir.dt.float8_e4m3fn_x4
+FP4X4 = mybir.dt.float4_e2m1fn_x4
+ALU = mybir.AluOpType
+COPY = mybir.ActivationFunctionType.Copy
+
+H_WIN = S + 16
+SEND_WIN = 352
+
+
+def tile_picked_cmixhaarsendhop_none_p_kernel(tc, x_words, x_scales, w1_words, w1_scales, gs, d_words, d_scales, offs, n1, n2, k1, k2, two, n3, n4, out):
+    nc = tc.nc
+    with ExitStack() as ctx:
+        lists = ctx.enter_context(tc.tile_pool(name="lists", bufs=1))
+        sb = ctx.enter_context(tc.tile_pool(name="sb", bufs=1))
+        psum = ctx.enter_context(tc.psum_pool(name="psum", bufs=1))
+
+        def load_list(name, src):
+            tile = lists.tile(list(src.shape), U16, name=name)
+            nc.sync.dma_start(out=tile[:], in_=src)
+            return tile
+
+        def new(name, shape, dtype):
+            return sb.tile(shape, dtype, name=name, align_bytes=64)
+
+        xs_win = new("xs_win", [P, T], U8)
+        ws_raw = new("ws_raw", [P, H], U8)
+        ds_win = new("ds_win", [P, G], U8)
+        ds_plane = new("ds_plane", [P, 2 * H], U8)
+        nc.vector.memset(ws_raw[:].bitcast(I32), 0)
+        nc.vector.memset(ds_win[:].bitcast(I32), 0)
+        nc.vector.memset(ds_plane[:].bitcast(I32), 0)
+        h_win = [new(f"h_win{t}", [P, H_WIN], F32) for t in range(PACK)]
+        for t in range(PACK):
+            nc.vector.memset(h_win[t][:, S:], 0.0)
+
+        xw_win = new("xw_win", [P, T], U32)
+        ww_raw = new("ww_raw", [P, 2 * H], U8)
+        dw_win = sb.tile([P, G], U32, name="dw_win", tag="table_then_z", align_bytes=64)
+        gain = new("gain", [P, PACK], F32)
+
+        for q in range(4):
+            rows = x_scales[0, 4 * q : 4 * q + 4, :].bitcast(I32).unsqueeze(0).broadcast_to([8, 4, T // 4])
+            (nc.sync if q % 2 else nc.scalar).dma_start(out=xs_win[32 * q : 32 * q + 32, :].bitcast(I32), in_=rows)
+        offs_l = load_list("offs_l", offs)
+        nc.scalar.dma_start(out=xw_win[:].bitcast(I32), in_=x_words[0].rearrange("p n t -> p (n t)").bitcast(I32))
+        two_l = load_list("two_l", two)
+        nc.sync.dma_start(out=ww_raw[:].bitcast(I32), in_=w1_words[0].bitcast(I32))
+        for q in range(4):
+            nc.sync.dma_start(out=ws_raw[32 * q : 32 * q + 4, :].bitcast(I32), in_=w1_scales[0, 4 * q : 4 * q + 4, :].bitcast(I32))
+        n1_l = load_list("n1_l", n1)
+        n2_l = load_list("n2_l", n2)
+        nc.sync.dma_start(out=ds_win[0:P:8, :].bitcast(I32), in_=d_scales[0].bitcast(I32))
+        k1_l = load_list("k1_l", k1)
+        k2_l = load_list("k2_l", k2)
+        nc.sync.dma_start(out=dw_win[:].bitcast(I32), in_=d_words[0].rearrange("p n t -> p (n t)").bitcast(I32))
+        nc.sync.dma_start(out=gain[:], in_=gs.rearrange("(p t) o -> p (t o)", t=PACK))
+        n3_l = load_list("n3_l", n3)
+        n4_l = load_list("n4_l", n4)
+
+        xq_s = new("xq_s", [P, S], U8)
+        xq_w = new("xq_w", [P, S], U32)
+        nc.vector.tensor_copy(out=xq_s[:], in_=xs_win[:].indirect(offs_l[:]))
+        nc.vector.tensor_copy(out=xq_w[:], in_=xw_win[:].indirect(offs_l[:]))
+
+        ww = [new(f"ww{t}", [P, 2 * P], U8) for t in range(PACK)]
+        ww_cols = ww_raw[:].bitcast(U16).rearrange("p (m t) -> p t m", t=PACK)
+        for t in range(PACK):
+            nc.scalar.copy(out=ww[t][:].bitcast(U16), in_=ww_cols[:, t, :])
+        ws_cols = ws_raw[:].rearrange("p (m t) -> p t m", t=PACK)
+        ws_first = new("ws_first", [P, P], U8)
+        ws_rest = new("ws_rest", [P, PACK - 1, P], U8)
+        nc.vector.tensor_copy(out=ws_first[:], in_=ws_cols[:, 0, :])
+        nc.vector.tensor_copy(out=ws_rest[:], in_=ws_cols[:, 1:, :])
+        ws = [ws_first[:]] + [ws_rest[:, t, :] for t in range(PACK - 1)]
+
+        y_win = [new(f"y_win{t}", [P, S], F32) for t in range(PACK)]
+        for t in range(PACK):
+            y_ps = psum.tile([P, S], F32, name=f"y_ps{t}")
+            nc.tensor.matmul_mx(out=y_ps[:], lhsT=ww[t][:].bitcast(FP4X4), lhsT_scale=ws[t], rhs=xq_w[:].bitcast(FP8X4), rhs_scale=xq_s[:], start=True, stop=True)
+            if t == 0:
+                nc.scalar.copy(out=y_win[t][:], in_=y_ps[:])
+            else:
+                nc.vector.tensor_copy(out=y_win[t][:], in_=y_ps[:])
+
+        pa = [new(f"pa{u}", [P, 2, W], F32) for u in range(2)]
+        pb = [new(f"pb{u}", [P, 2, W], F32) for u in range(2)]
+        total = [new(f"total{u}", [P, 2, W], F32) for u in range(2)]
+        diff = [new(f"diff{u}", [P, 2, W], F32) for u in range(2)]
+        for t in range(PACK):
+            nc.scalar.activation(out=pa[t // 2][:, t % 2, :], in_=y_win[t][:].indirect(n1_l[:]), func=COPY)
+            nc.scalar.activation(out=pb[t // 2][:, t % 2, :], in_=y_win[t][:].indirect(n2_l[:]), func=COPY)
+
+        def butterfly(u):
+            nc.vector.tensor_tensor(out=total[u][:], in0=pa[u][:], in1=pb[u][:], op=ALU.add)
+            nc.vector.tensor_tensor(out=diff[u][:], in0=pa[u][:], in1=pb[u][:], op=ALU.subtract)
+
+        butterfly(0)
+        x2_s = new("x2_s", [P, S], U8)
+        x2_w = new("x2_w", [P, S], U32)
+        nc.vector.tensor_copy(out=x2_s[:], in_=xs_win[:].indirect(two_l[:]))
+        nc.vector.tensor_copy(out=x2_w[:], in_=xw_win[:].indirect(two_l[:]))
+        ds_got = new("ds_got", [P, 2 * H], U8)
+        nc.vector.tensor_copy(out=ds_got[:, 0:H], in_=ds_win[:].indirect(k1_l[:]))
+        nc.vector.tensor_copy(out=ds_got[:, H:], in_=ds_win[:].indirect(k2_l[:]))
+        for r in range(4):
+            nc.sync.dma_start(out=ds_plane[r:P:32, :].bitcast(I32), in_=ds_got[8 * r : P : 32, :].bitcast(I32))
+        butterfly(1)
+        d1_w = new("d1_w", [P, H], U32)
+        d2_w = new("d2_w", [P, H], U32)
+        nc.vector.tensor_copy(out=d2_w[:], in_=dw_win[:].indirect(k2_l[:]))
+        nc.vector.tensor_copy(out=d1_w[:], in_=dw_win[:].indirect(k1_l[:]))
+
+        h_ps = [psum.tile([P, S], F32, name=f"h_ps{t}") for t in range(PACK)]
+        for t in range(PACK):
+            cols = slice(P * t, P * (t + 1))
+            nc.tensor.matmul_mx(out=h_ps[t][:], lhsT=d2_w[:, cols].bitcast(FP8X4), lhsT_scale=ds_plane[:, H + P * t : H + P * (t + 1)], rhs=x2_w[:].bitcast(FP8X4), rhs_scale=x2_s[:], start=True, stop=False)
+
+        z_win = [new(f"z_win{t}", [P, S], F32) for t in range(PACK)]
+        z_bf = sb.tile([P, S, PACK], BF16, name="z_bf", tag="table_then_z", align_bytes=64)
+        for pair in range(0, PACK, 2):
+            for t in (pair, pair + 1):
+                nc.scalar.activation(out=z_win[t][:].indirect(n1_l[:]), in_=total[t // 2][:, t % 2, :], func=COPY, scale=0.75)
+            for t in (pair, pair + 1):
+                nc.scalar.activation(out=z_win[t][:].indirect(n2_l[:]), in_=diff[t // 2][:, t % 2, :], func=COPY)
+                nc.vector.tensor_scalar(out=z_bf[:, :, t], in0=z_win[t][:], scalar1=gain[:, t : t + 1], scalar2=None, op0=ALU.mult)
+        z_w = new("z_w", [P, S], U32)
+        z_s = new("z_s", [P, S], U8)
+        nc.vector.quantize_mx(out=z_w[:].bitcast(FP8X4), scales=z_s[:], in_=z_bf[:].rearrange("p s t -> p (s t)"))
+
+        for t in range(PACK):
+            cols = slice(P * t, P * (t + 1))
+            nc.tensor.matmul_mx(out=h_ps[t][:], lhsT=d1_w[:, cols].bitcast(FP8X4), lhsT_scale=ds_plane[:, cols], rhs=z_w[:].bitcast(FP8X4), rhs_scale=z_s[:], start=False, stop=True)
+            if t == 0:
+                nc.scalar.activation(out=h_win[t][:, 0:S], in_=h_ps[t][:], func=COPY, scale=0.0625)
+            else:
+                nc.vector.tensor_scalar(out=h_win[t][:, 0:S], in0=h_ps[t][:], scalar1=0.0625, scalar2=None, op0=ALU.mult)
+
+        hop = [new(f"hop{t}", [P, S], F32) for t in range(PACK)]
+        st = [new(f"st{t}", [P, S], F32) for t in range(PACK)]
+        for t in range(PACK):
+            nc.scalar.activation(out=hop[t][:], in_=h_win[t][:].indirect(n3_l[:]), func=COPY)
+            nc.vector.tensor_tensor(out=st[t][:], in0=h_win[t][:, 0:S], in1=hop[t][:], op=ALU.max)
+        for t in range(PACK):
+            sent = new(f"sent{t}", [P, SEND_WIN], F32)
+            res = new(f"res{t}", [P, S], F32)
+            nc.scalar.activation(out=sent[:].indirect(n4_l[:]), in_=st[t][:], func=COPY)
+            nc.vector.tensor_tensor(out=res[:], in0=sent[:, 0:S], in1=h_win[t][:, 0:S], op=ALU.subtract)
+            nc.sync.dma_start(out=out[P * t : P * (t + 1), :], in_=res[:])

@@ -39,9 +39,8 @@ def tile_picked_cmixhaarsendhop_none_p_kernel(tc, x_words, x_scales, w1_words, w
 
         xs_win = new("xs_win", [P, T], U8)
         ws_raw = new("ws_raw", [P, H], U8)
-        ds_win = new("ds_win", [P, G], U8)
+        ds_win = sb.tile([P, G], U8, name="ds_win", tag="scales_then_x2", align_bytes=64)
         ds_plane = new("ds_plane", [P, 2 * H], U8)
-        nc.vector.memset(ws_raw[:].bitcast(I32), 0)
         nc.vector.memset(ds_win[:].bitcast(I32), 0)
         nc.vector.memset(ds_plane[:].bitcast(I32), 0)
         h_win = [new(f"h_win{t}", [P, H_WIN], F32) for t in range(PACK)]
@@ -50,23 +49,24 @@ def tile_picked_cmixhaarsendhop_none_p_kernel(tc, x_words, x_scales, w1_words, w
 
         xw_win = new("xw_win", [P, T], U32)
         ww_raw = new("ww_raw", [P, 2 * H], U8)
-        dw_win = sb.tile([P, G], U32, name="dw_win", tag="table_then_z", align_bytes=64)
+        dw_win = new("dw_win", [P, G], U32)
         gain = new("gain", [P, PACK], F32)
 
+        offs_l = load_list("offs_l", offs)
+        two_l = load_list("two_l", two)
         for q in range(4):
             rows = x_scales[0, 4 * q : 4 * q + 4, :].bitcast(I32).unsqueeze(0).broadcast_to([8, 4, T // 4])
-            (nc.sync if q % 2 else nc.scalar).dma_start(out=xs_win[32 * q : 32 * q + 32, :].bitcast(I32), in_=rows)
-        offs_l = load_list("offs_l", offs)
+            (nc.sync if q == 3 else nc.scalar).dma_start(out=xs_win[32 * q : 32 * q + 32, :].bitcast(I32), in_=rows)
         nc.scalar.dma_start(out=xw_win[:].bitcast(I32), in_=x_words[0].rearrange("p n t -> p (n t)").bitcast(I32))
-        two_l = load_list("two_l", two)
         nc.sync.dma_start(out=ww_raw[:].bitcast(I32), in_=w1_words[0].bitcast(I32))
         for q in range(4):
-            nc.sync.dma_start(out=ws_raw[32 * q : 32 * q + 4, :].bitcast(I32), in_=w1_scales[0, 4 * q : 4 * q + 4, :].bitcast(I32))
+            rows = w1_scales[0, 4 * q : 4 * q + 4, :].bitcast(I32).unsqueeze(0).broadcast_to([8, 4, H // 4])
+            nc.sync.dma_start(out=ws_raw[32 * q : 32 * q + 32, :].bitcast(I32), in_=rows)
         n1_l = load_list("n1_l", n1)
         n2_l = load_list("n2_l", n2)
         nc.sync.dma_start(out=ds_win[0:P:8, :].bitcast(I32), in_=d_scales[0].bitcast(I32))
-        k1_l = load_list("k1_l", k1)
         k2_l = load_list("k2_l", k2)
+        k1_l = load_list("k1_l", k1)
         nc.sync.dma_start(out=dw_win[:].bitcast(I32), in_=d_words[0].rearrange("p n t -> p (n t)").bitcast(I32))
         nc.sync.dma_start(out=gain[:], in_=gs.rearrange("(p t) o -> p (t o)", t=PACK))
         n3_l = load_list("n3_l", n3)
@@ -88,7 +88,7 @@ def tile_picked_cmixhaarsendhop_none_p_kernel(tc, x_words, x_scales, w1_words, w
         nc.vector.tensor_copy(out=ws_rest[:], in_=ws_cols[:, 1:, :])
         ws = [ws_first[:]] + [ws_rest[:, t, :] for t in range(PACK - 1)]
 
-        y_win = [new(f"y_win{t}", [P, S], F32) for t in range(PACK)]
+        y_win = [sb.tile([P, S], F32, name=f"y_win{t}", tag=f"y_then_z{t}", align_bytes=64) for t in range(PACK)]
         for t in range(PACK):
             y_ps = psum.tile([P, S], F32, name=f"y_ps{t}")
             nc.tensor.matmul_mx(out=y_ps[:], lhsT=ww[t][:].bitcast(FP4X4), lhsT_scale=ws[t], rhs=xq_w[:].bitcast(FP8X4), rhs_scale=xq_s[:], start=True, stop=True)
@@ -105,56 +105,85 @@ def tile_picked_cmixhaarsendhop_none_p_kernel(tc, x_words, x_scales, w1_words, w
             nc.scalar.activation(out=pa[t // 2][:, t % 2, :], in_=y_win[t][:].indirect(n1_l[:]), func=COPY)
             nc.scalar.activation(out=pb[t // 2][:, t % 2, :], in_=y_win[t][:].indirect(n2_l[:]), func=COPY)
 
+        x2_s = new("x2_s", [P, S], U8)
+        nc.vector.tensor_copy(out=x2_s[:], in_=xs_win[:].indirect(two_l[:]))
+
         def butterfly(u):
-            nc.vector.tensor_tensor(out=total[u][:], in0=pa[u][:], in1=pb[u][:], op=ALU.add)
-            nc.vector.tensor_tensor(out=diff[u][:], in0=pa[u][:], in1=pb[u][:], op=ALU.subtract)
+            nc.gpsimd.tensor_tensor(out=total[u][:], in0=pa[u][:], in1=pb[u][:], op=ALU.add)
+            nc.gpsimd.tensor_tensor(out=diff[u][:], in0=pa[u][:], in1=pb[u][:], op=ALU.subtract)
 
         butterfly(0)
-        x2_s = new("x2_s", [P, S], U8)
-        x2_w = new("x2_w", [P, S], U32)
-        nc.vector.tensor_copy(out=x2_s[:], in_=xs_win[:].indirect(two_l[:]))
-        nc.vector.tensor_copy(out=x2_w[:], in_=xw_win[:].indirect(two_l[:]))
-        ds_got = new("ds_got", [P, 2 * H], U8)
-        nc.vector.tensor_copy(out=ds_got[:, 0:H], in_=ds_win[:].indirect(k1_l[:]))
+        ds_got = sb.tile([P, 2 * H], U8, name="ds_got", tag="bytes_z_words", align_bytes=64)
         nc.vector.tensor_copy(out=ds_got[:, H:], in_=ds_win[:].indirect(k2_l[:]))
+        nc.vector.tensor_copy(out=ds_got[:, 0:H], in_=ds_win[:].indirect(k1_l[:]))
         for r in range(4):
             nc.sync.dma_start(out=ds_plane[r:P:32, :].bitcast(I32), in_=ds_got[8 * r : P : 32, :].bitcast(I32))
         butterfly(1)
-        d1_w = new("d1_w", [P, H], U32)
-        d2_w = new("d2_w", [P, H], U32)
-        nc.vector.tensor_copy(out=d2_w[:], in_=dw_win[:].indirect(k2_l[:]))
-        nc.vector.tensor_copy(out=d1_w[:], in_=dw_win[:].indirect(k1_l[:]))
+        x2_w = sb.tile([P, S], U32, name="x2_w", tag="scales_then_x2", align_bytes=64)
+        nc.vector.tensor_copy(out=x2_w[:], in_=xw_win[:].indirect(two_l[:]))
+        HALF = H // 2
 
-        h_ps = [psum.tile([P, S], F32, name=f"h_ps{t}") for t in range(PACK)]
-        for t in range(PACK):
-            cols = slice(P * t, P * (t + 1))
-            nc.tensor.matmul_mx(out=h_ps[t][:], lhsT=d2_w[:, cols].bitcast(FP8X4), lhsT_scale=ds_plane[:, H + P * t : H + P * (t + 1)], rhs=x2_w[:].bitcast(FP8X4), rhs_scale=x2_s[:], start=True, stop=False)
+        def pick_words(tile, half):
+            entries = slice(half * HALF // 16, (half + 1) * HALF // 16)
+            nc.vector.tensor_copy(out=tile[:, 1, :], in_=dw_win[:].indirect(k2_l[:, entries]))
+            nc.vector.tensor_copy(out=tile[:, 0, :], in_=dw_win[:].indirect(k1_l[:, entries]))
 
-        z_win = [new(f"z_win{t}", [P, S], F32) for t in range(PACK)]
-        z_bf = sb.tile([P, S, PACK], BF16, name="z_bf", tag="table_then_z", align_bytes=64)
+        h_ps = [psum.tile([P, S], F32, name=f"h_ps{t}") for t in range(1, PACK)]
+        h0_ps = [psum.tile([P, W], F32, name=f"h0_ps{c}", tag=f"h0_ps{c}" if c else "y_ps0") for c in range(2)]
+        halves = [slice(0, W), slice(W, S)]
+
+        def h_pass(acc, words, t, which, rhs, rhs_scale, cols):
+            nc.tensor.matmul_mx(
+                out=acc[:],
+                lhsT=words[:, which, P * (t % 2) : P * (t % 2 + 1)].bitcast(FP8X4),
+                lhsT_scale=ds_plane[:, which * H + P * t : which * H + P * (t + 1)],
+                rhs=rhs[:, cols].bitcast(FP8X4),
+                rhs_scale=rhs_scale[:, cols],
+                start=which == 1,
+                stop=which == 0,
+            )
+
+        d_lo = new("d_lo", [P, 2, HALF], U32)
+        pick_words(d_lo, 0)
+        for c in range(2):
+            h_pass(h0_ps[c], d_lo, 0, 1, x2_w, x2_s, halves[c])
+        h_pass(h_ps[0], d_lo, 1, 1, x2_w, x2_s, slice(0, S))
+
+        z_win = [sb.tile([P, S], F32, name=f"z_win{t}", tag=f"y_then_z{(t + 2) % PACK}", align_bytes=64) for t in range(PACK)]
+        z_bf = sb.tile([P, S, PACK], BF16, name="z_bf", tag="bytes_z_words", align_bytes=64)
         for pair in range(0, PACK, 2):
             for t in (pair, pair + 1):
                 nc.scalar.activation(out=z_win[t][:].indirect(n1_l[:]), in_=total[t // 2][:, t % 2, :], func=COPY, scale=0.75)
             for t in (pair, pair + 1):
                 nc.scalar.activation(out=z_win[t][:].indirect(n2_l[:]), in_=diff[t // 2][:, t % 2, :], func=COPY)
-                nc.vector.tensor_scalar(out=z_bf[:, :, t], in0=z_win[t][:], scalar1=gain[:, t : t + 1], scalar2=None, op0=ALU.mult)
+                for cols in halves if t == PACK - 1 else [slice(0, S)]:
+                    nc.vector.tensor_scalar(out=z_bf[:, cols, t], in0=z_win[t][:, cols], scalar1=gain[:, t : t + 1], scalar2=None, op0=ALU.mult)
         z_w = new("z_w", [P, S], U32)
         z_s = new("z_s", [P, S], U8)
-        nc.vector.quantize_mx(out=z_w[:].bitcast(FP8X4), scales=z_s[:], in_=z_bf[:].rearrange("p s t -> p (s t)"))
+        for cols in halves:
+            nc.vector.quantize_mx(out=z_w[:, cols].bitcast(FP8X4), scales=z_s[:, cols], in_=z_bf[:, cols, :].rearrange("p s t -> p (s t)"))
 
-        for t in range(PACK):
-            cols = slice(P * t, P * (t + 1))
-            nc.tensor.matmul_mx(out=h_ps[t][:], lhsT=d1_w[:, cols].bitcast(FP8X4), lhsT_scale=ds_plane[:, cols], rhs=z_w[:].bitcast(FP8X4), rhs_scale=z_s[:], start=False, stop=True)
-            if t == 0:
-                nc.scalar.activation(out=h_win[t][:, 0:S], in_=h_ps[t][:], func=COPY, scale=0.0625)
-            else:
-                nc.vector.tensor_scalar(out=h_win[t][:, 0:S], in0=h_ps[t][:], scalar1=0.0625, scalar2=None, op0=ALU.mult)
-
+        for c in range(2):
+            h_pass(h0_ps[c], d_lo, 0, 0, z_w, z_s, halves[c])
+            nc.scalar.activation(out=h_win[0][:, halves[c]], in_=h0_ps[c][:], func=COPY, scale=0.0625)
+        h_pass(h_ps[0], d_lo, 1, 0, z_w, z_s, slice(0, S))
+        nc.vector.tensor_scalar(out=h_win[1][:, 0:S], in0=h_ps[0][:], scalar1=0.0625, scalar2=None, op0=ALU.mult)
+        d_hi = sb.tile([P, 2, HALF], U32, name="d_hi", tag="bytes_z_words", align_bytes=64)
         hop = [new(f"hop{t}", [P, S], F32) for t in range(PACK)]
         st = [new(f"st{t}", [P, S], F32) for t in range(PACK)]
-        for t in range(PACK):
+
+        def larger(t):
             nc.scalar.activation(out=hop[t][:], in_=h_win[t][:].indirect(n3_l[:]), func=COPY)
             nc.vector.tensor_tensor(out=st[t][:], in0=h_win[t][:, 0:S], in1=hop[t][:], op=ALU.max)
+
+        larger(0)
+        larger(1)
+        pick_words(d_hi, 1)
+        for t in range(2, PACK):
+            h_pass(h_ps[t - 1], d_hi, t, 1, x2_w, x2_s, slice(0, S))
+            h_pass(h_ps[t - 1], d_hi, t, 0, z_w, z_s, slice(0, S))
+            nc.vector.tensor_scalar(out=h_win[t][:, 0:S], in0=h_ps[t - 1][:], scalar1=0.0625, scalar2=None, op0=ALU.mult)
+            larger(t)
         for t in range(PACK):
             sent = new(f"sent{t}", [P, SEND_WIN], F32)
             res = new(f"res{t}", [P, S], F32)

@@ -75,27 +75,30 @@ def tile_picked_cmixhaarsendhop_none_p_kernel(tc, x_words, x_scales, w1_words, w
         xq_s = new("xq_s", [P, S], U8)
         xq_w = new("xq_w", [P, S], U32)
         nc.vector.tensor_copy(out=xq_s[:], in_=xs_win[:].indirect(offs_l[:]))
-        nc.vector.tensor_copy(out=xq_w[:], in_=xw_win[:].indirect(offs_l[:]))
+        ws_cols = ws_raw[:].rearrange("p (m t) -> p t m", t=PACK)
+        ws_first = new("ws_first", [P, P], U8)
+        nc.vector.tensor_copy(out=ws_first[:], in_=ws_cols[:, 0, :])
+        halves = [slice(0, W), slice(W, S)]
+        for c in range(2):
+            nc.vector.tensor_copy(out=xq_w[:, halves[c]], in_=xw_win[:].indirect(offs_l[:, c * W // 16 : (c + 1) * W // 16]))
 
         ww = [new(f"ww{t}", [P, 2 * P], U8) for t in range(PACK)]
         ww_cols = ww_raw[:].bitcast(U16).rearrange("p (m t) -> p t m", t=PACK)
         for t in range(PACK):
             nc.scalar.copy(out=ww[t][:].bitcast(U16), in_=ww_cols[:, t, :])
-        ws_cols = ws_raw[:].rearrange("p (m t) -> p t m", t=PACK)
-        ws_first = new("ws_first", [P, P], U8)
         ws_rest = new("ws_rest", [P, PACK - 1, P], U8)
-        nc.vector.tensor_copy(out=ws_first[:], in_=ws_cols[:, 0, :])
         nc.vector.tensor_copy(out=ws_rest[:], in_=ws_cols[:, 1:, :])
         ws = [ws_first[:]] + [ws_rest[:, t, :] for t in range(PACK - 1)]
 
         y_win = [sb.tile([P, S], F32, name=f"y_win{t}", tag=f"y_then_z{t}", align_bytes=64) for t in range(PACK)]
-        for t in range(PACK):
+        for c in range(2):
+            y_ps = psum.tile([P, W], F32, name=f"y0_ps{c}", tag=f"first{c}")
+            nc.tensor.matmul_mx(out=y_ps[:], lhsT=ww[0][:].bitcast(FP4X4), lhsT_scale=ws[0], rhs=xq_w[:, halves[c]].bitcast(FP8X4), rhs_scale=xq_s[:, halves[c]], start=True, stop=True)
+            nc.scalar.copy(out=y_win[0][:, halves[c]], in_=y_ps[:])
+        for t in range(1, PACK):
             y_ps = psum.tile([P, S], F32, name=f"y_ps{t}")
             nc.tensor.matmul_mx(out=y_ps[:], lhsT=ww[t][:].bitcast(FP4X4), lhsT_scale=ws[t], rhs=xq_w[:].bitcast(FP8X4), rhs_scale=xq_s[:], start=True, stop=True)
-            if t == 0:
-                nc.scalar.copy(out=y_win[t][:], in_=y_ps[:])
-            else:
-                nc.vector.tensor_copy(out=y_win[t][:], in_=y_ps[:])
+            nc.vector.tensor_copy(out=y_win[t][:], in_=y_ps[:])
 
         pa = [new(f"pa{u}", [P, 2, W], F32) for u in range(2)]
         pb = [new(f"pb{u}", [P, 2, W], F32) for u in range(2)]
@@ -123,19 +126,18 @@ def tile_picked_cmixhaarsendhop_none_p_kernel(tc, x_words, x_scales, w1_words, w
         nc.vector.tensor_copy(out=x2_w[:], in_=xw_win[:].indirect(two_l[:]))
         HALF = H // 2
 
-        def pick_words(tile, half):
+        def pick_words(tiles, half):
             entries = slice(half * HALF // 16, (half + 1) * HALF // 16)
-            nc.vector.tensor_copy(out=tile[:, 1, :], in_=dw_win[:].indirect(k2_l[:, entries]))
-            nc.vector.tensor_copy(out=tile[:, 0, :], in_=dw_win[:].indirect(k1_l[:, entries]))
+            nc.vector.tensor_copy(out=tiles[1][:], in_=dw_win[:].indirect(k2_l[:, entries]))
+            nc.vector.tensor_copy(out=tiles[0][:], in_=dw_win[:].indirect(k1_l[:, entries]))
 
         h_ps = [psum.tile([P, S], F32, name=f"h_ps{t}") for t in range(1, PACK)]
-        h0_ps = [psum.tile([P, W], F32, name=f"h0_ps{c}", tag=f"h0_ps{c}" if c else "y_ps0") for c in range(2)]
-        halves = [slice(0, W), slice(W, S)]
+        h0_ps = [psum.tile([P, W], F32, name=f"h0_ps{c}", tag=f"first{c}") for c in range(2)]
 
         def h_pass(acc, words, t, which, rhs, rhs_scale, cols):
             nc.tensor.matmul_mx(
                 out=acc[:],
-                lhsT=words[:, which, P * (t % 2) : P * (t % 2 + 1)].bitcast(FP8X4),
+                lhsT=words[which][:, P * (t % 2) : P * (t % 2 + 1)].bitcast(FP8X4),
                 lhsT_scale=ds_plane[:, which * H + P * t : which * H + P * (t + 1)],
                 rhs=rhs[:, cols].bitcast(FP8X4),
                 rhs_scale=rhs_scale[:, cols],
@@ -143,7 +145,7 @@ def tile_picked_cmixhaarsendhop_none_p_kernel(tc, x_words, x_scales, w1_words, w
                 stop=which == 0,
             )
 
-        d_lo = new("d_lo", [P, 2, HALF], U32)
+        d_lo = [new(f"d_lo{i}", [P, HALF], U32) for i in range(2)]
         pick_words(d_lo, 0)
         for c in range(2):
             h_pass(h0_ps[c], d_lo, 0, 1, x2_w, x2_s, halves[c])
@@ -168,25 +170,29 @@ def tile_picked_cmixhaarsendhop_none_p_kernel(tc, x_words, x_scales, w1_words, w
             nc.scalar.activation(out=h_win[0][:, halves[c]], in_=h0_ps[c][:], func=COPY, scale=0.0625)
         h_pass(h_ps[0], d_lo, 1, 0, z_w, z_s, slice(0, S))
         nc.vector.tensor_scalar(out=h_win[1][:, 0:S], in0=h_ps[0][:], scalar1=0.0625, scalar2=None, op0=ALU.mult)
-        d_hi = sb.tile([P, 2, HALF], U32, name="d_hi", tag="bytes_z_words", align_bytes=64)
-        hop = [new(f"hop{t}", [P, S], F32) for t in range(PACK)]
-        st = [new(f"st{t}", [P, S], F32) for t in range(PACK)]
-
         def larger(t):
-            nc.scalar.activation(out=hop[t][:], in_=h_win[t][:].indirect(n3_l[:]), func=COPY)
-            nc.vector.tensor_tensor(out=st[t][:], in0=h_win[t][:, 0:S], in1=hop[t][:], op=ALU.max)
+            hop = sb.tile([P, S], F32, name=f"hop{t}", tag=f"hop{t}" if t < 2 else f"st{t - 2}", align_bytes=64)
+            st = sb.tile([P, S], F32, name=f"st{t}", tag=f"st{t}", align_bytes=64)
+            nc.scalar.activation(out=hop[:], in_=h_win[t][:].indirect(n3_l[:]), func=COPY)
+            nc.vector.tensor_tensor(out=st[:], in0=h_win[t][:, 0:S], in1=hop[:], op=ALU.max)
+            return st
 
-        larger(0)
-        larger(1)
+        def send(t, st):
+            sent = new(f"sent{t}", [P, SEND_WIN], F32)
+            res = new(f"res{t}", [P, S], F32)
+            nc.scalar.activation(out=sent[:].indirect(n4_l[:]), in_=st[:], func=COPY)
+            nc.vector.tensor_tensor(out=res[:], in0=sent[:, 0:S], in1=h_win[t][:, 0:S], op=ALU.subtract)
+            nc.sync.dma_start(out=out[P * t : P * (t + 1), :], in_=res[:])
+
+        st_lo = [larger(t) for t in range(2)]
+        d_hi = [sb.tile([P, HALF], U32, name=f"d_hi{i}", tag=["hop0", "bytes_z_words"][i], align_bytes=64) for i in range(2)]
         pick_words(d_hi, 1)
         for t in range(2, PACK):
             h_pass(h_ps[t - 1], d_hi, t, 1, x2_w, x2_s, slice(0, S))
             h_pass(h_ps[t - 1], d_hi, t, 0, z_w, z_s, slice(0, S))
             nc.vector.tensor_scalar(out=h_win[t][:, 0:S], in0=h_ps[t - 1][:], scalar1=0.0625, scalar2=None, op0=ALU.mult)
-            larger(t)
-        for t in range(PACK):
-            sent = new(f"sent{t}", [P, SEND_WIN], F32)
-            res = new(f"res{t}", [P, S], F32)
-            nc.scalar.activation(out=sent[:].indirect(n4_l[:]), in_=st[t][:], func=COPY)
-            nc.vector.tensor_tensor(out=res[:], in0=sent[:, 0:S], in1=h_win[t][:, 0:S], op=ALU.subtract)
-            nc.sync.dma_start(out=out[P * t : P * (t + 1), :], in_=res[:])
+        for t in range(2):
+            send(t, st_lo[t])
+        st_hi = [larger(t) for t in range(2, PACK)]
+        for t in range(2, PACK):
+            send(t, st_hi[t - 2])

@@ -41,6 +41,7 @@ def tile_picked_cmixhaarsendhop_none_p_kernel(tc, x_words, x_scales, w1_words, w
         ws_raw = new("ws_raw", [P, H], U8)
         ds_win = sb.tile([P, G], U8, name="ds_win", tag="scales_then_x2", align_bytes=64)
         ds_plane = new("ds_plane", [P, 2 * H], U8)
+        nc.vector.memset(ws_raw[:].bitcast(I32), 0)
         nc.vector.memset(ds_win[:].bitcast(I32), 0)
         nc.vector.memset(ds_plane[:].bitcast(I32), 0)
         h_win = [new(f"h_win{t}", [P, H_WIN], F32) for t in range(PACK)]
@@ -53,20 +54,19 @@ def tile_picked_cmixhaarsendhop_none_p_kernel(tc, x_words, x_scales, w1_words, w
         gain = new("gain", [P, PACK], F32)
 
         offs_l = load_list("offs_l", offs)
-        two_l = load_list("two_l", two)
         for q in range(4):
             rows = x_scales[0, 4 * q : 4 * q + 4, :].bitcast(I32).unsqueeze(0).broadcast_to([8, 4, T // 4])
-            (nc.sync if q == 3 else nc.scalar).dma_start(out=xs_win[32 * q : 32 * q + 32, :].bitcast(I32), in_=rows)
+            (nc.sync if q % 2 else nc.scalar).dma_start(out=xs_win[32 * q : 32 * q + 32, :].bitcast(I32), in_=rows)
         nc.scalar.dma_start(out=xw_win[:].bitcast(I32), in_=x_words[0].rearrange("p n t -> p (n t)").bitcast(I32))
         nc.sync.dma_start(out=ww_raw[:].bitcast(I32), in_=w1_words[0].bitcast(I32))
         for q in range(4):
-            rows = w1_scales[0, 4 * q : 4 * q + 4, :].bitcast(I32).unsqueeze(0).broadcast_to([8, 4, H // 4])
-            nc.sync.dma_start(out=ws_raw[32 * q : 32 * q + 32, :].bitcast(I32), in_=rows)
+            nc.sync.dma_start(out=ws_raw[32 * q : 32 * q + 4, :].bitcast(I32), in_=w1_scales[0, 4 * q : 4 * q + 4, :].bitcast(I32))
         n1_l = load_list("n1_l", n1)
         n2_l = load_list("n2_l", n2)
         nc.sync.dma_start(out=ds_win[0:P:8, :].bitcast(I32), in_=d_scales[0].bitcast(I32))
         k2_l = load_list("k2_l", k2)
         k1_l = load_list("k1_l", k1)
+        two_l = load_list("two_l", two)
         nc.sync.dma_start(out=dw_win[:].bitcast(I32), in_=d_words[0].rearrange("p n t -> p (n t)").bitcast(I32))
         nc.sync.dma_start(out=gain[:], in_=gs.rearrange("(p t) o -> p (t o)", t=PACK))
         n3_l = load_list("n3_l", n3)
@@ -108,8 +108,6 @@ def tile_picked_cmixhaarsendhop_none_p_kernel(tc, x_words, x_scales, w1_words, w
             nc.scalar.activation(out=pa[t // 2][:, t % 2, :], in_=y_win[t][:].indirect(n1_l[:]), func=COPY)
             nc.scalar.activation(out=pb[t // 2][:, t % 2, :], in_=y_win[t][:].indirect(n2_l[:]), func=COPY)
 
-        x2_s = new("x2_s", [P, S], U8)
-        nc.vector.tensor_copy(out=x2_s[:], in_=xs_win[:].indirect(two_l[:]))
 
         def butterfly(u):
             nc.gpsimd.tensor_tensor(out=total[u][:], in0=pa[u][:], in1=pb[u][:], op=ALU.add)
@@ -122,6 +120,8 @@ def tile_picked_cmixhaarsendhop_none_p_kernel(tc, x_words, x_scales, w1_words, w
         for r in range(4):
             nc.sync.dma_start(out=ds_plane[r:P:32, :].bitcast(I32), in_=ds_got[8 * r : P : 32, :].bitcast(I32))
         butterfly(1)
+        x2_s = new("x2_s", [P, S], U8)
+        nc.vector.tensor_copy(out=x2_s[:], in_=xs_win[:].indirect(two_l[:]))
         x2_w = sb.tile([P, S], U32, name="x2_w", tag="scales_then_x2", align_bytes=64)
         nc.vector.tensor_copy(out=x2_w[:], in_=xw_win[:].indirect(two_l[:]))
         HALF = H // 2

from contextlib import ExitStack

import concourse.mybir as mybir

K, T, S, H, W, G = 512, 1024, 256, 512, 128, 2048
P = 128
PACK = 4
FLOPS = 3 * 2 * K * H * S

F32 = mybir.dt.float32
BF16 = mybir.dt.bfloat16
I32 = mybir.dt.int32
U32 = mybir.dt.uint32
U16 = mybir.dt.uint16
U8 = mybir.dt.uint8
FP8X4 = mybir.dt.float8_e4m3fn_x4
FP4X4 = mybir.dt.float4_e2m1fn_x4
ALU = mybir.AluOpType
COPY = mybir.ActivationFunctionType.Copy

H_WIN = S + 16
SEND_WIN = 352


def tile_picked_cmixhaarsendhop_none_p_kernel(tc, x_words, x_scales, w1_words, w1_scales, gs, d_words, d_scales, offs, n1, n2, k1, k2, two, n3, n4, out):
    nc = tc.nc
    with ExitStack() as ctx:
        lists = ctx.enter_context(tc.tile_pool(name="lists", bufs=1))
        sb = ctx.enter_context(tc.tile_pool(name="sb", bufs=1))
        psum = ctx.enter_context(tc.psum_pool(name="psum", bufs=1))

        def load_list(name, src):
            tile = lists.tile(list(src.shape), U16, name=name)
            nc.sync.dma_start(out=tile[:], in_=src)
            return tile

        def new(name, shape, dtype):
            return sb.tile(shape, dtype, name=name, align_bytes=64)

        xs_win = new("xs_win", [P, T], U8)
        ws_raw = new("ws_raw", [P, H], U8)
        ds_win = sb.tile([P, G], U8, name="ds_win", tag="scales_then_x2", align_bytes=64)
        ds_plane = new("ds_plane", [P, 2 * H], U8)
        nc.vector.memset(ws_raw[:].bitcast(I32), 0)
        nc.vector.memset(ds_win[:].bitcast(I32), 0)
        nc.vector.memset(ds_plane[:].bitcast(I32), 0)
        h_win = [new(f"h_win{t}", [P, H_WIN], F32) for t in range(PACK)]
        for t in range(PACK):
            nc.vector.memset(h_win[t][:, S:], 0.0)

        xw_win = new("xw_win", [P, T], U32)
        ww_raw = new("ww_raw", [P, 2 * H], U8)
        dw_win = new("dw_win", [P, G], U32)
        gain = new("gain", [P, PACK], F32)

        offs_l = load_list("offs_l", offs)
        for q in range(4):
            rows = x_scales[0, 4 * q : 4 * q + 4, :].bitcast(I32).unsqueeze(0).broadcast_to([8, 4, T // 4])
            (nc.sync if q % 2 else nc.scalar).dma_start(out=xs_win[32 * q : 32 * q + 32, :].bitcast(I32), in_=rows)
        nc.scalar.dma_start(out=xw_win[:].bitcast(I32), in_=x_words[0].rearrange("p n t -> p (n t)").bitcast(I32))
        nc.sync.dma_start(out=ww_raw[:].bitcast(I32), in_=w1_words[0].bitcast(I32))
        for q in range(4):
            nc.sync.dma_start(out=ws_raw[32 * q : 32 * q + 4, :].bitcast(I32), in_=w1_scales[0, 4 * q : 4 * q + 4, :].bitcast(I32))
        n1_l = load_list("n1_l", n1)
        n2_l = load_list("n2_l", n2)
        nc.sync.dma_start(out=ds_win[0:P:8, :].bitcast(I32), in_=d_scales[0].bitcast(I32))
        k2_l = load_list("k2_l", k2)
        k1_l = load_list("k1_l", k1)
        two_l = load_list("two_l", two)
        nc.sync.dma_start(out=dw_win[:].bitcast(I32), in_=d_words[0].rearrange("p n t -> p (n t)").bitcast(I32))
        nc.sync.dma_start(out=gain[:], in_=gs.rearrange("(p t) o -> p (t o)", t=PACK))
        n3_l = load_list("n3_l", n3)
        n4_l = load_list("n4_l", n4)

        xq_s = new("xq_s", [P, S], U8)
        xq_w = new("xq_w", [P, S], U32)
        nc.vector.tensor_copy(out=xq_s[:], in_=xs_win[:].indirect(offs_l[:]))
        ws_cols = ws_raw[:].rearrange("p (m t) -> p t m", t=PACK)
        ws_first = new("ws_first", [P, P], U8)
        nc.vector.tensor_copy(out=ws_first[:], in_=ws_cols[:, 0, :])
        halves = [slice(0, W), slice(W, S)]
        for c in range(2):
            nc.vector.tensor_copy(out=xq_w[:, halves[c]], in_=xw_win[:].indirect(offs_l[:, c * W // 16 : (c + 1) * W // 16]))

        ww = [new(f"ww{t}", [P, 2 * P], U8) for t in range(PACK)]
        ww_cols = ww_raw[:].bitcast(U16).rearrange("p (m t) -> p t m", t=PACK)
        for t in range(PACK):
            nc.scalar.copy(out=ww[t][:].bitcast(U16), in_=ww_cols[:, t, :])
        ws_rest = new("ws_rest", [P, PACK - 1, P], U8)
        nc.vector.tensor_copy(out=ws_rest[:], in_=ws_cols[:, 1:, :])
        ws = [ws_first[:]] + [ws_rest[:, t, :] for t in range(PACK - 1)]

        y_win = [sb.tile([P, S], F32, name=f"y_win{t}", tag=f"y_then_z{t}", align_bytes=64) for t in range(PACK)]
        for c in range(2):
            y_ps = psum.tile([P, W], F32, name=f"y0_ps{c}", tag=f"first{c}")
            nc.tensor.matmul_mx(out=y_ps[:], lhsT=ww[0][:].bitcast(FP4X4), lhsT_scale=ws[0], rhs=xq_w[:, halves[c]].bitcast(FP8X4), rhs_scale=xq_s[:, halves[c]], start=True, stop=True)
            nc.scalar.copy(out=y_win[0][:, halves[c]], in_=y_ps[:])
        for t in range(1, PACK):
            y_ps = psum.tile([P, S], F32, name=f"y_ps{t}")
            nc.tensor.matmul_mx(out=y_ps[:], lhsT=ww[t][:].bitcast(FP4X4), lhsT_scale=ws[t], rhs=xq_w[:].bitcast(FP8X4), rhs_scale=xq_s[:], start=True, stop=True)
            nc.vector.tensor_copy(out=y_win[t][:], in_=y_ps[:])

        pa = [new(f"pa{u}", [P, 2, W], F32) for u in range(2)]
        pb = [new(f"pb{u}", [P, 2, W], F32) for u in range(2)]
        total = [new(f"total{u}", [P, 2, W], F32) for u in range(2)]
        diff = [new(f"diff{u}", [P, 2, W], F32) for u in range(2)]
        for t in range(PACK):
            nc.scalar.activation(out=pa[t // 2][:, t % 2, :], in_=y_win[t][:].indirect(n1_l[:]), func=COPY)
            nc.scalar.activation(out=pb[t // 2][:, t % 2, :], in_=y_win[t][:].indirect(n2_l[:]), func=COPY)


        def butterfly(u):
            nc.gpsimd.tensor_tensor(out=total[u][:], in0=pa[u][:], in1=pb[u][:], op=ALU.add)
            nc.gpsimd.tensor_tensor(out=diff[u][:], in0=pa[u][:], in1=pb[u][:], op=ALU.subtract)

        butterfly(0)
        ds_got = sb.tile([P, 2 * H], U8, name="ds_got", tag="bytes_z_words", align_bytes=64)
        nc.vector.tensor_copy(out=ds_got[:, H:], in_=ds_win[:].indirect(k2_l[:]))
        nc.vector.tensor_copy(out=ds_got[:, 0:H], in_=ds_win[:].indirect(k1_l[:]))
        for r in range(4):
            nc.sync.dma_start(out=ds_plane[r:P:32, :].bitcast(I32), in_=ds_got[8 * r : P : 32, :].bitcast(I32))
        butterfly(1)
        x2_s = new("x2_s", [P, S], U8)
        nc.vector.tensor_copy(out=x2_s[:], in_=xs_win[:].indirect(two_l[:]))
        x2_w = sb.tile([P, S], U32, name="x2_w", tag="scales_then_x2", align_bytes=64)
        nc.vector.tensor_copy(out=x2_w[:], in_=xw_win[:].indirect(two_l[:]))
        HALF = H // 2

        def pick_words(tiles, half):
            entries = slice(half * HALF // 16, (half + 1) * HALF // 16)
            nc.vector.tensor_copy(out=tiles[1][:], in_=dw_win[:].indirect(k2_l[:, entries]))
            nc.vector.tensor_copy(out=tiles[0][:], in_=dw_win[:].indirect(k1_l[:, entries]))

        h_ps = [psum.tile([P, S], F32, name=f"h_ps{t}") for t in range(1, PACK)]
        h0_ps = [psum.tile([P, W], F32, name=f"h0_ps{c}", tag=f"first{c}") for c in range(2)]

        def h_pass(acc, words, t, which, rhs, rhs_scale, cols):
            nc.tensor.matmul_mx(
                out=acc[:],
                lhsT=words[which][:, P * (t % 2) : P * (t % 2 + 1)].bitcast(FP8X4),
                lhsT_scale=ds_plane[:, which * H + P * t : which * H + P * (t + 1)],
                rhs=rhs[:, cols].bitcast(FP8X4),
                rhs_scale=rhs_scale[:, cols],
                start=which == 1,
                stop=which == 0,
            )

        d_lo = [new(f"d_lo{i}", [P, HALF], U32) for i in range(2)]
        pick_words(d_lo, 0)
        for c in range(2):
            h_pass(h0_ps[c], d_lo, 0, 1, x2_w, x2_s, halves[c])
        h_pass(h_ps[0], d_lo, 1, 1, x2_w, x2_s, slice(0, S))

        z_win = [sb.tile([P, S], F32, name=f"z_win{t}", tag=f"y_then_z{(t + 2) % PACK}", align_bytes=64) for t in range(PACK)]
        z_bf = sb.tile([P, S, PACK], BF16, name="z_bf", tag="bytes_z_words", align_bytes=64)
        for pair in range(0, PACK, 2):
            for t in (pair, pair + 1):
                nc.scalar.activation(out=z_win[t][:].indirect(n1_l[:]), in_=total[t // 2][:, t % 2, :], func=COPY, scale=0.75)
            for t in (pair, pair + 1):
                nc.scalar.activation(out=z_win[t][:].indirect(n2_l[:]), in_=diff[t // 2][:, t % 2, :], func=COPY)
                for cols in halves if t == PACK - 1 else [slice(0, S)]:
                    nc.vector.tensor_scalar(out=z_bf[:, cols, t], in0=z_win[t][:, cols], scalar1=gain[:, t : t + 1], scalar2=None, op0=ALU.mult)
        z_w = new("z_w", [P, S], U32)
        z_s = new("z_s", [P, S], U8)
        for cols in halves:
            nc.vector.quantize_mx(out=z_w[:, cols].bitcast(FP8X4), scales=z_s[:, cols], in_=z_bf[:, cols, :].rearrange("p s t -> p (s t)"))

        for c in range(2):
            h_pass(h0_ps[c], d_lo, 0, 0, z_w, z_s, halves[c])
            nc.scalar.activation(out=h_win[0][:, halves[c]], in_=h0_ps[c][:], func=COPY, scale=0.0625)
        h_pass(h_ps[0], d_lo, 1, 0, z_w, z_s, slice(0, S))
        nc.vector.tensor_scalar(out=h_win[1][:, 0:S], in0=h_ps[0][:], scalar1=0.0625, scalar2=None, op0=ALU.mult)
        def larger(t):
            hop = sb.tile([P, S], F32, name=f"hop{t}", tag=f"hop{t}" if t < 2 else f"st{t - 2}", align_bytes=64)
            st = sb.tile([P, S], F32, name=f"st{t}", tag=f"st{t}", align_bytes=64)
            nc.scalar.activation(out=hop[:], in_=h_win[t][:].indirect(n3_l[:]), func=COPY)
            nc.vector.tensor_tensor(out=st[:], in0=h_win[t][:, 0:S], in1=hop[:], op=ALU.max)
            return st

        def send(t, st):
            sent = new(f"sent{t}", [P, SEND_WIN], F32)
            res = new(f"res{t}", [P, S], F32)
            nc.scalar.activation(out=sent[:].indirect(n4_l[:]), in_=st[:], func=COPY)
            nc.vector.tensor_tensor(out=res[:], in0=sent[:, 0:S], in1=h_win[t][:, 0:S], op=ALU.subtract)
            nc.sync.dma_start(out=out[P * t : P * (t + 1), :], in_=res[:])

        st_lo = [larger(t) for t in range(2)]
        d_hi = [sb.tile([P, HALF], U32, name=f"d_hi{i}", tag=["hop0", "bytes_z_words"][i], align_bytes=64) for i in range(2)]
        pick_words(d_hi, 1)
        for t in range(2, PACK):
            h_pass(h_ps[t - 1], d_hi, t, 1, x2_w, x2_s, slice(0, S))
            h_pass(h_ps[t - 1], d_hi, t, 0, z_w, z_s, slice(0, S))
            nc.vector.tensor_scalar(out=h_win[t][:, 0:S], in0=h_ps[t - 1][:], scalar1=0.0625, scalar2=None, op0=ALU.mult)
        for t in range(2):
            send(t, st_lo[t])
        st_hi = [larger(t) for t in range(2, PACK)]
        for t in range(2, PACK):
            send(t, st_hi[t - 2])
